import numpy as np
import ml_dtypes


def mxq(x, axis, fmt="e4m3"):
    dtype, down = {"e4m3": (ml_dtypes.float8_e4m3fn, 7), "e5m2": (ml_dtypes.float8_e5m2, 14)}[fmt]
    v = np.moveaxis(np.asarray(x, np.float32).astype(ml_dtypes.bfloat16).astype(np.float64), axis, -1)
    blocks = v.reshape(v.shape[:-1] + (-1, 32))
    amax = np.abs(blocks).max(-1, keepdims=True)
    byte = np.maximum(np.where(amax > 0, np.frexp(amax)[1] - 1 + 127, 0) - down, 1)
    scale = np.exp2(byte - 127.0)
    codes = (blocks / scale).astype(np.float32).astype(dtype).astype(np.float64)
    return np.moveaxis((codes * scale).reshape(v.shape), -1, axis)


WIDE = False


def mx_kscale(k):
    if not WIDE:
        return np.ones(k)
    levels = np.array([10, -10, 5, -5, 0])
    if k % 512:
        return np.exp2(np.random.permutation(np.resize(levels, k // 32))).repeat(32)
    a = np.empty((k // 512, 16))
    for p in range(k // 512):
        a[p, :8] = np.random.permutation(np.resize(levels, 8))
        for g in range(8):
            far = levels[np.abs(levels - a[p, g]) >= 10]
            a[p, g + 8] = far[np.random.randint(len(far))]
    return np.exp2(a.ravel()).repeat(32)


BF16 = ml_dtypes.bfloat16


def bf(x):
    return np.asarray(x, np.float32).astype(BF16)


def f64(x):
    return np.asarray(x).astype(np.float64)

def planes(Y):
    n, m = Y.shape
    b = f64(bf(Y)).reshape(n // 32, 32, m)
    amax = np.abs(b).max(1)
    byte = np.clip(np.where(amax > 0, np.frexp(amax)[1] - 1 + 127 - 7, 1), 1, 254)
    codes = (b * np.exp2(127.0 - byte)[:, None, :]).reshape(n, m).astype(np.float32).astype(ml_dtypes.float8_e4m3fn).view(np.uint8)
    words = codes.reshape(n // 512, 128, 4, m).transpose(0, 1, 3, 2)
    return np.ascontiguousarray(words), np.ascontiguousarray(byte.astype(np.uint8).reshape(n // 512, 16, m))


N, C = 1024, 1024


def setup_inputs():
    s = mx_kscale(N)
    h = np.random.standard_normal((N, N)) / np.sqrt(N)
    g = 1.0 + 0.1 * np.random.standard_normal(N)
    v = np.random.standard_normal(N) * 0.5
    x = np.random.standard_normal((N, C))
    return {"h": bf(h / s[None, :]), "g": bf(g * s), "v": bf(v), "x": bf(x)}


def core(h, g, v, x):
    h, g, v, x = f64(h), f64(g), f64(v), f64(x)
    c = 0.75
    e = 1.75
    a0 = -2.3
    s1 = e / (a0 - c)
    s2 = 1.0 / (2.0 / s1 - s1)
    u = v - c
    hq = mxq(h, 1, "e4m3")
    xg = g[:, None] * x
    p1 = hq @ mxq(xg, 0, "e4m3")
    y1 = (s1 / e) * (p1 + u[:, None] * x)
    yg = g[:, None] * y1
    p2 = hq @ mxq(yg, 0, "e4m3")
    y2 = (2.0 * s2 / e) * (p2 + u[:, None] * y1) - s1 * s2 * x
    return y2


def reference(h, g, v, x):
    R_out = core(h, g, v, x)
    words, scales = planes(R_out.T)
    return R_out, words, scales

@@ -1,0 +1,325 @@
+import concourse.mybir as mybir
+from concourse.masks import make_identity
+
+F32 = mybir.dt.float32
+BF16 = mybir.dt.bfloat16
+U32 = mybir.dt.uint32
+I32 = mybir.dt.int32
+U8 = mybir.dt.uint8
+FP8X4 = mybir.dt.float8_e4m3fn_x4
+ADD = mybir.AluOpType.add
+MULT = mybir.AluOpType.mult
+SUB = mybir.AluOpType.subtract
+COPY = mybir.ActivationFunctionType.Copy
+
+N = 1024
+P = 128
+S1 = 1.75 / (-2.3 - 0.75)
+S2 = 1.0 / (2.0 / S1 - S1)
+A = S1 / 1.75
+B = 2.0 * S2 / 1.75
+FLOPS = 2 * 2 * N * N * N
+
+UN = [(0, 0), (0, 1), (1, 0), (1, 1)]
+XS = dict(zip(UN, "ssss"))
+ILX = dict(zip(UN, "vvss"))
+ILY = dict(zip(UN, "vvvv"))
+CAST = dict(zip(UN, ("ssss", "ssss", "ssss", "svsv")))
+CPO = dict(zip(UN, "ssss"))
+
+
+def tile_chebyshevfilteredsubspaceblock_x1_kernel(tc, h, g, v, x, out, words, scales):
+    nc = tc.nc
+    with tc.tile_pool(name="keep", bufs=1) as keep, tc.tile_pool(name="work", bufs=2) as work, tc.psum_pool(
+        name="acc", bufs=6
+    ) as acc, tc.psum_pool(name="turn", bufs=2) as turn, tc.manual_schedule():
+        gt = keep.tile([P, 2, 16], BF16, name="gt")
+        vt = keep.tile([P, 2, 16], BF16, name="vt")
+        nc.scalar.dma_start(out=gt[:, :, 0:4], in_=g.rearrange("(G p t) -> p G t", p=P, t=4))
+        nc.scalar.dma_start(out=vt[:, :, 0:4], in_=v.rearrange("(G p t) -> p G t", p=P, t=4))
+        xr = {}
+        hr = {}
+
+        def load_x(s, G):
+            t = keep.tile([P, 4, 512], BF16, name=f"xr{s}{G}", align_bytes=64)
+            nc.sync.dma_start(
+                out=t[:],
+                in_=x[512 * G : 512 * G + 512, 512 * s : 512 * s + 512].rearrange("(p t) c -> p t c", t=4),
+            )
+            xr[s, G] = t
+
+        def load_h(G, T):
+            t = keep.tile([P, 2, N], BF16, name=f"hr{G}{T}", align_bytes=64)
+            nc.sync.dma_start(
+                out=t[:],
+                in_=h[512 * G : 512 * G + 512, :].rearrange("(p t) k -> p t k", t=4)[:, 2 * T : 2 * T + 2, :],
+            )
+            hr[G, T] = t
+
+        load_x(0, 0)
+        load_x(0, 1)
+        load_h(0, 0)
+        load_h(0, 1)
+        load_h(1, 0)
+        load_h(1, 1)
+        load_x(1, 0)
+        load_x(1, 1)
+
+        ga = keep.tile([P, 2, 4], F32, name="ga")
+        u = keep.tile([P, 2, 4], F32, name="u")
+        bau = keep.tile([P, 2, 4], F32, name="bau")
+        gp = nc.gpsimd
+        ident = keep.tile([P, P], F32, name="ident")
+        make_identity(nc, ident[:])
+        gp.tensor_scalar(out=ga[:], in0=gt[:, :, 0:4], scalar1=A, scalar2=0.0, op0=MULT, op1=ADD)
+        gp.tensor_scalar(out=u[:], in0=vt[:, :, 0:4], scalar1=0.75, scalar2=0.0, op0=SUB, op1=ADD)
+        gp.tensor_scalar(out=bau[:], in0=u[:], scalar1=A * B, scalar2=0.0, op0=MULT, op1=ADD)
+
+        xc, xs, hc, hs, yc, ys = {}, {}, {}, {}, {}, {}
+        xg, xi, hg, z, res, zg, yi, yb, go, psc, b1, b2 = {}, {}, {}, {}, {}, {}, {}, {}, {}, {}, {}, {}
+
+        def quant(src, width, name):
+            c = keep.tile([P, width], U32, name=f"c{name}", align_bytes=64)
+            s = keep.tile([P, width], U8, name=f"s{name}", align_bytes=64)
+            nc.vector.quantize_mx(out=c[:].bitcast(FP8X4), scales=s[:], in_=src)
+            return c, s
+
+        def cp(eng, o, i):
+            if eng == "s":
+                nc.scalar.copy(out=o, in_=i)
+            elif eng == "g":
+                nc.gpsimd.tensor_scalar(out=o, in0=i, scalar1=1.0, scalar2=0.0, op0=MULT, op1=ADD)
+            else:
+                nc.vector.tensor_copy(out=o, in_=i)
+
+        def scale_x(s, G):
+            t = work.tile([P, 4, 512], BF16, name="xg", bufs=4, align_bytes=64)
+            for j in range(4):
+                nc.vector.tensor_scalar_mul(out=t[:, j, :], in0=xr[s, G][:, j, :], scalar1=gt[:, G, j : j + 1])
+            xg[s, G] = t
+
+        def weave(eng, t, src):
+            cp(eng, t[:].rearrange("p (c i) t -> p c t i", i=4), src[:].rearrange("p t (c i) -> p c t i", i=4))
+
+        def il_x(s, G):
+            xi[s, G] = t = work.tile([P, 512, 4], BF16, name="xi", bufs=3, align_bytes=64)
+            weave(ILX[s, G], t, xg[s, G])
+
+        def q_x(s, G):
+            xc[s, G], xs[s, G] = quant(xi[s, G][:].rearrange("p c t -> p (c t)"), 512, f"x{s}{G}")
+
+        def make_xs(s, G):
+            res[s, G] = t = keep.tile([P, 4, 512], F32, name=f"res{s}{G}")
+            e = XS[s, G]
+            if e == "s":
+                nc.scalar.activation(out=t[:], in_=xr[s, G][:], func=COPY, scale=-S1 * S2)
+            elif e == "g":
+                for j in range(4):
+                    nc.gpsimd.tensor_scalar(
+                        out=t[:, j, :], in0=xr[s, G][:, j, :], scalar1=-S1 * S2, scalar2=0.0, op0=MULT, op1=ADD
+                    )
+            else:
+                nc.vector.tensor_scalar_mul(out=t[:], in0=xr[s, G][:], scalar1=-S1 * S2)
+
+        def turn_h(G, T):
+            hg[G, T] = t = work.tile([P, 2, 2, P, 4], BF16, name="hg", align_bytes=64)
+            tv = t[:].bitcast(F32)
+            for tt in range(2):
+                w = hr[G, T][:, tt, :].bitcast(F32)
+                b = acc.tile([P, 512], F32, name="pb")
+                for kk in range(2):
+                    for uu in range(2):
+                        col = 256 * kk + 128 * uu
+                        nc.tensor.transpose(b[:, col : col + 128], w[:, 256 * kk + uu : 256 * kk + 256 : 2], ident[:])
+                nc.scalar.copy(out=tv[:, tt, :, :, :], in_=b[:].rearrange("p (k u i) -> p k i u", k=2, u=2))
+
+        def q_h(G, T):
+            hc[G, T], hs[G, T] = quant(hg[G, T][:].rearrange("p a k i t -> p (a k i t)"), 512, f"h{G}{T}")
+
+        def mm(s, G, t, bc, bs):
+            b = acc.tile([P, 512], F32, name="pb")
+            T, tt = divmod(t, 2)
+            for kk in range(2):
+                cols = slice(256 * tt + 128 * kk, 256 * tt + 128 * kk + 128)
+                nc.tensor.matmul_mx(
+                    out=b[:],
+                    lhsT=hc[G, T][:, cols].bitcast(FP8X4),
+                    lhsT_scale=hs[G, T][:, cols],
+                    rhs=bc[s, kk][:].bitcast(FP8X4),
+                    rhs_scale=bs[s, kk][:],
+                    start=(kk == 0),
+                    stop=(kk == 1),
+                )
+            return b
+
+        def mm1(s, G, ts=range(4)):
+            for t in ts:
+                b1[s, G, t] = mm(s, G, t, xc, xs)
+
+        def mm2(s, G, ts=range(4)):
+            for t in ts:
+                b2[s, G, t] = mm(s, G, t, yc, ys)
+
+        def add1(s, G, t):
+            if t == 0:
+                z[s, G] = keep.tile([P, 4, 512], F32, name=f"z{s}{G}")
+                zg[s, G] = work.tile([P, 4, 512], BF16, name="zg", align_bytes=64)
+            nc.vector.scalar_tensor_tensor(
+                out=z[s, G][:, t, :],
+                in0=xr[s, G][:, t, :],
+                scalar=u[:, G, t : t + 1],
+                in1=b1[s, G, t][:],
+                op0=MULT,
+                op1=ADD,
+            )
+
+        def gain(s, G, t):
+            nc.scalar.activation(
+                out=zg[s, G][:, t, :], in_=z[s, G][:, t, :], func=COPY, scale=ga[:, G, t : t + 1]
+            )
+
+        def il_y(s, G):
+            yi[s, G] = t = work.tile([P, 512, 4], BF16, name="yi", align_bytes=64)
+            weave(ILY[s, G], t, zg[s, G])
+
+        def q_y(s, G):
+            yc[s, G], ys[s, G] = quant(yi[s, G][:].rearrange("p c t -> p (c t)"), 512, f"y{s}{G}")
+
+        def w(s, G):
+            for t in range(4):
+                r = res[s, G][:, t, :]
+                nc.vector.scalar_tensor_tensor(
+                    out=r, in0=z[s, G][:, t, :], scalar=bau[:, G, t : t + 1], in1=r, op0=MULT, op1=ADD
+                )
+
+        def add2(s, G, t):
+            r = res[s, G][:, t, :]
+            nc.vector.scalar_tensor_tensor(out=r, in0=b2[s, G, t][:], scalar=B, in1=r, op0=MULT, op1=ADD)
+            nc.sync.dma_start(
+                out=out[512 * G : 512 * G + 512, 512 * s : 512 * s + 512].rearrange("(p t) c -> p t c", t=4)[:, t, :],
+                in_=r,
+            )
+
+        def cast(s, G, t):
+            yb[s, G, t] = b = work.tile([P, 2, P, 2], BF16, name="yb", bufs=4, align_bytes=64)
+            cp(CAST[s, G][t], b[:], res[s, G][:, t, :].rearrange("p (m u e) -> p u m e", u=2, e=2))
+
+        def turn_y(s, G, T):
+            b = turn.tile([P, 2, 2, P], F32, name="tb")
+            for tt in range(2):
+                wv = yb[s, G, 2 * T + tt][:].rearrange("p u m e -> p (u m e)").bitcast(F32)
+                for uu in range(2):
+                    nc.tensor.transpose(b[:, tt, uu, :], wv[:, 128 * uu : 128 * uu + 128], ident[:])
+            if T == 0:
+                go[s, G] = work.tile([P, P, 2, 2, 4], BF16, name="go", align_bytes=64)
+            cp(CPO[s, G], go[s, G][:].bitcast(F32)[:, :, T, :, :], b[:].rearrange("p a u m -> p m a u"))
+
+        def q_o(s, G):
+            if G == 0:
+                psc[s] = keep.tile([P, N], U8, name=f"psc{s}", align_bytes=64)
+            c = keep.tile([P, 512], U32, name=f"oc{s}{G}", align_bytes=64)
+            nc.vector.quantize_mx(
+                out=c[:].bitcast(FP8X4),
+                scales=psc[s][:, 512 * G : 512 * G + 512],
+                in_=go[s, G][:].rearrange("p m a b t -> p (m a b t)"),
+            )
+            nc.sync.dma_start(
+                out=words.rearrange("g p m t -> g p (m t)")[s].bitcast(I32)[:, 512 * G : 512 * G + 512],
+                in_=c[:].bitcast(I32),
+            )
+            if G == 1:
+                for Q in range(4):
+                    nc.sync.dma_start(
+                        out=scales[s, 4 * Q : 4 * Q + 4, :].bitcast(I32),
+                        in_=psc[s][32 * Q : 32 * Q + 4, :].bitcast(I32),
+                    )
+
+        make_xs(0, 0)
+        scale_x(0, 0)
+        scale_x(0, 1)
+        il_x(0, 0)
+        il_x(0, 1)
+        q_x(0, 0)
+        q_x(0, 1)
+        turn_h(0, 0)
+        turn_h(0, 1)
+        q_h(0, 0)
+        turn_h(1, 0)
+        mm1(0, 0, (0, 1))
+        q_h(0, 1)
+        turn_h(1, 1)
+        mm1(0, 0, (2, 3))
+        add1(0, 0, 0)
+        q_h(1, 0)
+        add1(0, 0, 1)
+        mm1(0, 1, (0, 1))
+        q_h(1, 1)
+        mm1(0, 1, (2, 3))
+        gain(0, 0, 0)
+        gain(0, 0, 1)
+        for t in (2, 3):
+            add1(0, 0, t)
+            gain(0, 0, t)
+        scale_x(1, 0)
+        for t in (0, 1, 2, 3):
+            add1(0, 1, t)
+            gain(0, 1, t)
+        scale_x(1, 1)
+        il_x(1, 0)
+        il_y(0, 0)
+        il_x(1, 1)
+        make_xs(0, 1)
+        q_y(0, 0)
+        il_y(0, 1)
+        w(0, 0)
+        q_y(0, 1)
+        q_x(1, 0)
+        q_x(1, 1)
+        mm1(1, 0)
+        mm2(0, 0)
+        for t in range(4):
+            add1(1, 0, t)
+            gain(1, 0, t)
+        mm1(1, 1)
+        for t in range(4):
+            add1(1, 1, t)
+            gain(1, 1, t)
+        il_y(1, 0)
+        for t in range(4):
+            add2(0, 0, t)
+            cast(0, 0, t)
+        q_y(1, 0)
+        mm2(0, 1)
+        il_y(1, 1)
+        turn_y(0, 0, 0)
+        turn_y(0, 0, 1)
+        w(0, 1)
+        q_y(1, 1)
+        make_xs(1, 0)
+        for t in range(4):
+            add2(0, 1, t)
+            cast(0, 1, t)
+        make_xs(1, 1)
+        q_o(0, 0)
+        turn_y(0, 1, 0)
+        turn_y(0, 1, 1)
+        mm2(1, 0)
+        w(1, 0)
+        q_o(0, 1)
+        for t in range(4):
+            add2(1, 0, t)
+            cast(1, 0, t)
+            if t == 1:
+                mm2(1, 1, (0, 1))
+                turn_y(1, 0, 0)
+        mm2(1, 1, (2, 3))
+        turn_y(1, 0, 1)
+        w(1, 1)
+        for t in range(4):
+            add2(1, 1, t)
+            cast(1, 1, t)
+            if t % 2:
+                turn_y(1, 1, t // 2)
+            if t == 1:
+                q_o(1, 0)
+        q_o(1, 1)

@@ -14,312 +14,344 @@ COPY = mybir.ActivationFunctionType.Copy
 
 N = 1024
 P = 128
-S1 = 1.75 / (-2.3 - 0.75)
+HALF = 512
+
+C_SHIFT = 0.75
+E_WIDTH = 1.75
+S1 = E_WIDTH / (-2.3 - C_SHIFT)
 S2 = 1.0 / (2.0 / S1 - S1)
-A = S1 / 1.75
-B = 2.0 * S2 / 1.75
+A = S1 / E_WIDTH
+B = 2.0 * S2 / E_WIDTH
+D = -S1 * S2
+
 FLOPS = 2 * 2 * N * N * N
 
-UN = [(0, 0), (0, 1), (1, 0), (1, 1)]
-XS = dict(zip(UN, "ssss"))
-ILX = dict(zip(UN, "vvss"))
-ILY = dict(zip(UN, "vvvv"))
-CAST = dict(zip(UN, ("ssss", "ssss", "ssss", "svsv")))
-CPO = dict(zip(UN, "ssss"))
+ALL_T = (0, 1, 2, 3)
+PAIRS = (0, 1)
 
 
 def tile_chebyshevfilteredsubspaceblock_x1_kernel(tc, h, g, v, x, out, words, scales):
     nc = tc.nc
-    with tc.tile_pool(name="keep", bufs=1) as keep, tc.tile_pool(name="work", bufs=2) as work, tc.psum_pool(
-        name="acc", bufs=6
-    ) as acc, tc.psum_pool(name="turn", bufs=2) as turn, tc.manual_schedule():
-        gt = keep.tile([P, 2, 16], BF16, name="gt")
-        vt = keep.tile([P, 2, 16], BF16, name="vt")
-        nc.scalar.dma_start(out=gt[:, :, 0:4], in_=g.rearrange("(G p t) -> p G t", p=P, t=4))
-        nc.scalar.dma_start(out=vt[:, :, 0:4], in_=v.rearrange("(G p t) -> p G t", p=P, t=4))
-        xr = {}
-        hr = {}
+    with tc.tile_pool(name="keep", bufs=1) as keep, tc.tile_pool(name="work", bufs=3) as work, tc.psum_pool(
+        name="bank", bufs=8
+    ) as bank, tc.manual_schedule():
+        x_raw, x_gain, x_woven, x_codes, x_scales = {}, {}, {}, {}, {}
+        h_raw, h_bank, h_woven, h_codes, h_scales = {}, {}, {}, {}, {}
+        bank1, z, z_gain, y_woven, y_codes, y_scales = {}, {}, {}, {}, {}, {}
+        bank2, total, rounded, p_bank, p_woven, p_scales = {}, {}, {}, {}, {}, {}
 
-        def load_x(s, G):
-            t = keep.tile([P, 4, 512], BF16, name=f"xr{s}{G}", align_bytes=64)
+        def columns(half):
+            return slice(HALF * half, HALF * half + HALF)
+
+        def rows(group):
+            return slice(512 * group, 512 * group + 512)
+
+
+        g_rows = keep.tile([P, 2, 16], BF16, name="g_rows")
+        v_rows = keep.tile([P, 2, 16], BF16, name="v_rows")
+
+        def load_x(group, pair):
+            if group not in x_raw:
+                x_raw[group] = keep.tile([P, 4, N], BF16, name=f"x_raw{group}", align_bytes=64)
+            two = slice(2 * pair, 2 * pair + 2)
             nc.sync.dma_start(
-                out=t[:],
-                in_=x[512 * G : 512 * G + 512, 512 * s : 512 * s + 512].rearrange("(p t) c -> p t c", t=4),
+                out=x_raw[group][:, two, :], in_=x[rows(group), :].rearrange("(p t) c -> p t c", t=4)[:, two, :]
             )
-            xr[s, G] = t
 
-        def load_h(G, T):
-            t = keep.tile([P, 2, N], BF16, name=f"hr{G}{T}", align_bytes=64)
+        def load_h(group, pair):
+            h_raw[group, pair] = keep.tile([P, 2, N], BF16, name=f"h_raw{group}{pair}", align_bytes=64)
             nc.sync.dma_start(
-                out=t[:],
-                in_=h[512 * G : 512 * G + 512, :].rearrange("(p t) k -> p t k", t=4)[:, 2 * T : 2 * T + 2, :],
+                out=h_raw[group, pair][:],
+                in_=h[rows(group), :].rearrange("(p t) k -> p t k", t=4)[:, 2 * pair : 2 * pair + 2, :],
             )
-            hr[G, T] = t
 
+        nc.scalar.dma_start(out=g_rows[:, :, 0:4], in_=g.rearrange("(G p t) -> p G t", p=P, t=4))
         load_x(0, 0)
         load_x(0, 1)
-        load_h(0, 0)
-        load_h(0, 1)
         load_h(1, 0)
-        load_h(1, 1)
+        load_h(0, 0)
         load_x(1, 0)
         load_x(1, 1)
+        load_h(1, 1)
+        load_h(0, 1)
+        nc.sync.dma_start(out=v_rows[:, :, 0:4], in_=v.rearrange("(G p t) -> p G t", p=P, t=4))
 
-        ga = keep.tile([P, 2, 4], F32, name="ga")
+
+        ag = keep.tile([P, 2, 4], F32, name="ag")
         u = keep.tile([P, 2, 4], F32, name="u")
-        bau = keep.tile([P, 2, 4], F32, name="bau")
-        gp = nc.gpsimd
-        ident = keep.tile([P, P], F32, name="ident")
-        make_identity(nc, ident[:])
-        gp.tensor_scalar(out=ga[:], in0=gt[:, :, 0:4], scalar1=A, scalar2=0.0, op0=MULT, op1=ADD)
-        gp.tensor_scalar(out=u[:], in0=vt[:, :, 0:4], scalar1=0.75, scalar2=0.0, op0=SUB, op1=ADD)
-        gp.tensor_scalar(out=bau[:], in0=u[:], scalar1=A * B, scalar2=0.0, op0=MULT, op1=ADD)
+        abu = keep.tile([P, 2, 4], F32, name="abu")
+        identity = keep.tile([P, P], F32, name="identity")
+        make_identity(nc, identity[:])
+        nc.gpsimd.tensor_scalar(out=ag[:], in0=g_rows[:, :, 0:4], scalar1=A, scalar2=0.0, op0=MULT, op1=ADD)
+        nc.gpsimd.tensor_scalar(out=u[:], in0=v_rows[:, :, 0:4], scalar1=C_SHIFT, scalar2=0.0, op0=SUB, op1=ADD)
+        nc.gpsimd.tensor_scalar(out=abu[:], in0=u[:], scalar1=A * B, scalar2=0.0, op0=MULT, op1=ADD)
 
-        xc, xs, hc, hs, yc, ys = {}, {}, {}, {}, {}, {}
-        xg, xi, hg, z, res, zg, yi, yb, go, psc, b1, b2 = {}, {}, {}, {}, {}, {}, {}, {}, {}, {}, {}, {}
 
-        def quant(src, width, name):
-            c = keep.tile([P, width], U32, name=f"c{name}", align_bytes=64)
-            s = keep.tile([P, width], U8, name=f"s{name}", align_bytes=64)
-            nc.vector.quantize_mx(out=c[:].bitcast(FP8X4), scales=s[:], in_=src)
-            return c, s
+        def quantize(source, name):
+            codes = keep.tile([P, 512], U32, name=f"codes_{name}", align_bytes=64)
+            scale = keep.tile([P, 512], U8, name=f"scales_{name}", align_bytes=64)
+            nc.vector.quantize_mx(out=codes[:].bitcast(FP8X4), scales=scale[:], in_=source)
+            return codes, scale
 
-        def cp(eng, o, i):
-            if eng == "s":
-                nc.scalar.copy(out=o, in_=i)
-            elif eng == "g":
-                nc.gpsimd.tensor_scalar(out=o, in0=i, scalar1=1.0, scalar2=0.0, op0=MULT, op1=ADD)
-            else:
-                nc.vector.tensor_copy(out=o, in_=i)
+        def weave(copy, woven, source):
+            copy(
+                out=woven[:].rearrange("p (c i) t -> p c t i", i=4),
+                in_=source.rearrange("p t (c i) -> p c t i", i=4),
+            )
 
-        def scale_x(s, G):
-            t = work.tile([P, 4, 512], BF16, name="xg", bufs=4, align_bytes=64)
-            for j in range(4):
-                nc.vector.tensor_scalar_mul(out=t[:, j, :], in0=xr[s, G][:, j, :], scalar1=gt[:, G, j : j + 1])
-            xg[s, G] = t
-
-        def weave(eng, t, src):
-            cp(eng, t[:].rearrange("p (c i) t -> p c t i", i=4), src[:].rearrange("p t (c i) -> p c t i", i=4))
-
-        def il_x(s, G):
-            xi[s, G] = t = work.tile([P, 512, 4], BF16, name="xi", bufs=3, align_bytes=64)
-            weave(ILX[s, G], t, xg[s, G])
-
-        def q_x(s, G):
-            xc[s, G], xs[s, G] = quant(xi[s, G][:].rearrange("p c t -> p (c t)"), 512, f"x{s}{G}")
-
-        def make_xs(s, G):
-            res[s, G] = t = keep.tile([P, 4, 512], F32, name=f"res{s}{G}")
-            e = XS[s, G]
-            if e == "s":
-                nc.scalar.activation(out=t[:], in_=xr[s, G][:], func=COPY, scale=-S1 * S2)
-            elif e == "g":
-                for j in range(4):
-                    nc.gpsimd.tensor_scalar(
-                        out=t[:, j, :], in0=xr[s, G][:, j, :], scalar1=-S1 * S2, scalar2=0.0, op0=MULT, op1=ADD
-                    )
-            else:
-                nc.vector.tensor_scalar_mul(out=t[:], in0=xr[s, G][:], scalar1=-S1 * S2)
-
-        def turn_h(G, T):
-            hg[G, T] = t = work.tile([P, 2, 2, P, 4], BF16, name="hg", align_bytes=64)
-            tv = t[:].bitcast(F32)
-            for tt in range(2):
-                w = hr[G, T][:, tt, :].bitcast(F32)
-                b = acc.tile([P, 512], F32, name="pb")
-                for kk in range(2):
-                    for uu in range(2):
-                        col = 256 * kk + 128 * uu
-                        nc.tensor.transpose(b[:, col : col + 128], w[:, 256 * kk + uu : 256 * kk + 256 : 2], ident[:])
-                nc.scalar.copy(out=tv[:, tt, :, :, :], in_=b[:].rearrange("p (k u i) -> p k i u", k=2, u=2))
-
-        def q_h(G, T):
-            hc[G, T], hs[G, T] = quant(hg[G, T][:].rearrange("p a k i t -> p (a k i t)"), 512, f"h{G}{T}")
-
-        def mm(s, G, t, bc, bs):
-            b = acc.tile([P, 512], F32, name="pb")
-            T, tt = divmod(t, 2)
-            for kk in range(2):
-                cols = slice(256 * tt + 128 * kk, 256 * tt + 128 * kk + 128)
-                nc.tensor.matmul_mx(
-                    out=b[:],
-                    lhsT=hc[G, T][:, cols].bitcast(FP8X4),
-                    lhsT_scale=hs[G, T][:, cols],
-                    rhs=bc[s, kk][:].bitcast(FP8X4),
-                    rhs_scale=bs[s, kk][:],
-                    start=(kk == 0),
-                    stop=(kk == 1),
+        def gain_x(group, pair):
+            if group not in x_gain:
+                x_gain[group] = keep.tile([P, 4, N], BF16, name=f"x_gain{group}", align_bytes=64)
+            for t in (2 * pair, 2 * pair + 1):
+                nc.vector.tensor_scalar_mul(
+                    out=x_gain[group][:, t, :], in0=x_raw[group][:, t, :], scalar1=g_rows[:, group, t : t + 1]
                 )
-            return b
 
-        def mm1(s, G, ts=range(4)):
-            for t in ts:
-                b1[s, G, t] = mm(s, G, t, xc, xs)
+        def weave_x(half, group, copy):
+            x_woven[half, group] = work.tile([P, HALF, 4], BF16, name="x_woven", align_bytes=64)
+            weave(copy, x_woven[half, group], x_gain[group][:, :, columns(half)])
 
-        def mm2(s, G, ts=range(4)):
-            for t in ts:
-                b2[s, G, t] = mm(s, G, t, yc, ys)
+        def quantize_x(half, group):
+            x_codes[half, group], x_scales[half, group] = quantize(
+                x_woven[half, group][:].rearrange("p c t -> p (c t)"), f"x{half}{group}"
+            )
 
-        def add1(s, G, t):
-            if t == 0:
-                z[s, G] = keep.tile([P, 4, 512], F32, name=f"z{s}{G}")
-                zg[s, G] = work.tile([P, 4, 512], BF16, name="zg", align_bytes=64)
+        def start_total(group, pair):
+            if group not in total:
+                total[group] = keep.tile([P, 4, N], F32, name=f"total{group}")
+            two = slice(2 * pair, 2 * pair + 2)
+            nc.scalar.activation(out=total[group][:, two, :], in_=x_raw[group][:, two, :], func=COPY, scale=D)
+
+        def turn_h(group, pair, i):
+            row_words = h_raw[group, pair][:, i, :].bitcast(F32)
+            turned = bank.tile([P, 512], F32, name="bank")
+            h_bank[group, pair, i] = turned
+            for k_group in range(2):
+                for w in range(2):
+                    at = 256 * k_group + 128 * w
+                    nc.tensor.transpose(
+                        turned[:, at : at + P],
+                        row_words[:, 256 * k_group + w : 256 * k_group + 256 : 2],
+                        identity[:],
+                    )
+
+        def copy_h(group, pair, i):
+            if (group, pair) not in h_woven:
+                h_woven[group, pair] = work.tile([P, 2, 2, P, 4], BF16, name="h_woven", align_bytes=64)
+            nc.scalar.copy(
+                out=h_woven[group, pair][:].bitcast(F32)[:, i, :, :, :],
+                in_=h_bank[group, pair, i][:].rearrange("p (k w r) -> p k r w", k=2, w=2),
+            )
+
+        def quantize_h(group, pair):
+            h_codes[group, pair], h_scales[group, pair] = quantize(
+                h_woven[group, pair][:].rearrange("p i k r t -> p (i k r t)"), f"h{group}{pair}"
+            )
+
+        def product(half, group, t, codes, scale):
+            acc = bank.tile([P, HALF], F32, name="bank")
+            pair, i = divmod(t, 2)
+            for k_group in range(2):
+                at = 256 * i + 128 * k_group
+                nc.tensor.matmul_mx(
+                    out=acc[:],
+                    lhsT=h_codes[group, pair][:, at : at + P].bitcast(FP8X4),
+                    lhsT_scale=h_scales[group, pair][:, at : at + P],
+                    rhs=codes[half, k_group][:].bitcast(FP8X4),
+                    rhs_scale=scale[half, k_group][:],
+                    start=(k_group == 0),
+                    stop=(k_group == 1),
+                )
+            return acc
+
+        def first_product(half, group, t):
+            bank1[half, group, t] = product(half, group, t, x_codes, x_scales)
+
+        def first_sum(half, group, t):
+            if group not in z:
+                z[group] = keep.tile([P, 4, N], F32, name=f"z{group}")
             nc.vector.scalar_tensor_tensor(
-                out=z[s, G][:, t, :],
-                in0=xr[s, G][:, t, :],
-                scalar=u[:, G, t : t + 1],
-                in1=b1[s, G, t][:],
+                out=z[group][:, t, columns(half)],
+                in0=x_raw[group][:, t, columns(half)],
+                scalar=u[:, group, t : t + 1],
+                in1=bank1[half, group, t][:],
                 op0=MULT,
                 op1=ADD,
             )
 
-        def gain(s, G, t):
+        def gain_z(half, group, t):
+            if (half, group) not in z_gain:
+                z_gain[half, group] = work.tile([P, 4, HALF], BF16, name="z_gain", align_bytes=64)
             nc.scalar.activation(
-                out=zg[s, G][:, t, :], in_=z[s, G][:, t, :], func=COPY, scale=ga[:, G, t : t + 1]
+                out=z_gain[half, group][:, t, :],
+                in_=z[group][:, t, columns(half)],
+                func=COPY,
+                scale=ag[:, group, t : t + 1],
             )
 
-        def il_y(s, G):
-            yi[s, G] = t = work.tile([P, 512, 4], BF16, name="yi", align_bytes=64)
-            weave(ILY[s, G], t, zg[s, G])
+        def weave_y(half, group):
+            y_woven[half, group] = work.tile([P, HALF, 4], BF16, name="y_woven", align_bytes=64)
+            weave(nc.scalar.copy, y_woven[half, group], z_gain[half, group][:])
 
-        def q_y(s, G):
-            yc[s, G], ys[s, G] = quant(yi[s, G][:].rearrange("p c t -> p (c t)"), 512, f"y{s}{G}")
+        def quantize_y(half, group):
+            y_codes[half, group], y_scales[half, group] = quantize(
+                y_woven[half, group][:].rearrange("p c t -> p (c t)"), f"y{half}{group}"
+            )
 
-        def w(s, G):
-            for t in range(4):
-                r = res[s, G][:, t, :]
-                nc.vector.scalar_tensor_tensor(
-                    out=r, in0=z[s, G][:, t, :], scalar=bau[:, G, t : t + 1], in1=r, op0=MULT, op1=ADD
-                )
+        def extend_total(group, t):
+            nc.vector.scalar_tensor_tensor(
+                out=total[group][:, t, :],
+                in0=z[group][:, t, :],
+                scalar=abu[:, group, t : t + 1],
+                in1=total[group][:, t, :],
+                op0=MULT,
+                op1=ADD,
+            )
 
-        def add2(s, G, t):
-            r = res[s, G][:, t, :]
-            nc.vector.scalar_tensor_tensor(out=r, in0=b2[s, G, t][:], scalar=B, in1=r, op0=MULT, op1=ADD)
+        def second_product(half, group, t):
+            bank2[half, group, t] = product(half, group, t, y_codes, y_scales)
+
+        def finish(half, group, t):
+            result = total[group][:, t, columns(half)]
+            nc.vector.scalar_tensor_tensor(
+                out=result, in0=bank2[half, group, t][:], scalar=B, in1=result, op0=MULT, op1=ADD
+            )
             nc.sync.dma_start(
-                out=out[512 * G : 512 * G + 512, 512 * s : 512 * s + 512].rearrange("(p t) c -> p t c", t=4)[:, t, :],
-                in_=r,
+                out=out[rows(group), columns(half)].rearrange("(p t) c -> p t c", t=4)[:, t, :], in_=result
             )
 
-        def cast(s, G, t):
-            yb[s, G, t] = b = work.tile([P, 2, P, 2], BF16, name="yb", bufs=4, align_bytes=64)
-            cp(CAST[s, G][t], b[:], res[s, G][:, t, :].rearrange("p (m u e) -> p u m e", u=2, e=2))
+        def round_out(half, group, t, engine):
+            rounded[half, group, t] = work.tile([P, 2, P, 2], BF16, name="rounded", bufs=8, align_bytes=64)
+            to = rounded[half, group, t][:]
+            source = total[group][:, t, columns(half)].rearrange("p (m w e) -> p w m e", w=2, e=2)
+            if engine == "gpsimd":
+                nc.gpsimd.tensor_scalar(out=to, in0=source, scalar1=1.0, scalar2=0.0, op0=MULT, op1=ADD)
+            elif engine == "vector":
+                nc.vector.tensor_copy(out=to, in_=source)
+            else:
+                nc.scalar.copy(out=to, in_=source)
 
-        def turn_y(s, G, T):
-            b = turn.tile([P, 2, 2, P], F32, name="tb")
-            for tt in range(2):
-                wv = yb[s, G, 2 * T + tt][:].rearrange("p u m e -> p (u m e)").bitcast(F32)
-                for uu in range(2):
-                    nc.tensor.transpose(b[:, tt, uu, :], wv[:, 128 * uu : 128 * uu + 128], ident[:])
-            if T == 0:
-                go[s, G] = work.tile([P, P, 2, 2, 4], BF16, name="go", align_bytes=64)
-            cp(CPO[s, G], go[s, G][:].bitcast(F32)[:, :, T, :, :], b[:].rearrange("p a u m -> p m a u"))
+        def turn_out(half, group, pair):
+            turned = bank.tile([P, 2, 2, P], F32, name="bank")
+            p_bank[half, group, pair] = turned
+            for i in range(2):
+                pair_words = rounded[half, group, 2 * pair + i][:].rearrange("p w m e -> p (w m e)").bitcast(F32)
+                for w in range(2):
+                    nc.tensor.transpose(turned[:, i, w, :], pair_words[:, P * w : P * w + P], identity[:])
 
-        def q_o(s, G):
-            if G == 0:
-                psc[s] = keep.tile([P, N], U8, name=f"psc{s}", align_bytes=64)
-            c = keep.tile([P, 512], U32, name=f"oc{s}{G}", align_bytes=64)
+        def copy_out(half, group, pair):
+            if (half, group) not in p_woven:
+                p_woven[half, group] = work.tile([P, P, 2, 2, 4], BF16, name="p_woven", bufs=2, align_bytes=64)
+            nc.scalar.copy(
+                out=p_woven[half, group][:].bitcast(F32)[:, :, pair, :, :],
+                in_=p_bank[half, group, pair][:].rearrange("m i w r -> m r i w"),
+            )
+
+        def quantize_out(half, group, scale_queue):
+            if half not in p_scales:
+                p_scales[half] = keep.tile([P, N], U8, name=f"scales_p{half}", align_bytes=64)
+            codes = keep.tile([P, 512], U32, name=f"codes_p{half}{group}", align_bytes=64)
             nc.vector.quantize_mx(
-                out=c[:].bitcast(FP8X4),
-                scales=psc[s][:, 512 * G : 512 * G + 512],
-                in_=go[s, G][:].rearrange("p m a b t -> p (m a b t)"),
+                out=codes[:].bitcast(FP8X4),
+                scales=p_scales[half][:, rows(group)],
+                in_=p_woven[half, group][:].rearrange("m r q i t -> m (r q i t)"),
             )
             nc.sync.dma_start(
-                out=words.rearrange("g p m t -> g p (m t)")[s].bitcast(I32)[:, 512 * G : 512 * G + 512],
-                in_=c[:].bitcast(I32),
+                out=words.rearrange("G p r t -> G p (r t)")[half].bitcast(I32)[:, rows(group)],
+                in_=codes[:].bitcast(I32),
             )
-            if G == 1:
-                for Q in range(4):
-                    nc.sync.dma_start(
-                        out=scales[s, 4 * Q : 4 * Q + 4, :].bitcast(I32),
-                        in_=psc[s][32 * Q : 32 * Q + 4, :].bitcast(I32),
+            if group == 1:
+                for q in range(4):
+                    scale_queue.dma_start(
+                        out=scales[half, 4 * q : 4 * q + 4, :].bitcast(I32),
+                        in_=p_scales[half][32 * q : 32 * q + 4, :].bitcast(I32),
                     )
 
-        make_xs(0, 0)
-        scale_x(0, 0)
-        scale_x(0, 1)
-        il_x(0, 0)
-        il_x(0, 1)
-        q_x(0, 0)
-        q_x(0, 1)
-        turn_h(0, 0)
-        turn_h(0, 1)
-        q_h(0, 0)
-        turn_h(1, 0)
-        mm1(0, 0, (0, 1))
-        q_h(0, 1)
-        turn_h(1, 1)
-        mm1(0, 0, (2, 3))
-        add1(0, 0, 0)
-        q_h(1, 0)
-        add1(0, 0, 1)
-        mm1(0, 1, (0, 1))
-        q_h(1, 1)
-        mm1(0, 1, (2, 3))
-        gain(0, 0, 0)
-        gain(0, 0, 1)
-        for t in (2, 3):
-            add1(0, 0, t)
-            gain(0, 0, t)
-        scale_x(1, 0)
-        for t in (0, 1, 2, 3):
-            add1(0, 1, t)
-            gain(0, 1, t)
-        scale_x(1, 1)
-        il_x(1, 0)
-        il_y(0, 0)
-        il_x(1, 1)
-        make_xs(0, 1)
-        q_y(0, 0)
-        il_y(0, 1)
-        w(0, 0)
-        q_y(0, 1)
-        q_x(1, 0)
-        q_x(1, 1)
-        mm1(1, 0)
-        mm2(0, 0)
-        for t in range(4):
-            add1(1, 0, t)
-            gain(1, 0, t)
-        mm1(1, 1)
-        for t in range(4):
-            add1(1, 1, t)
-            gain(1, 1, t)
-        il_y(1, 0)
-        for t in range(4):
-            add2(0, 0, t)
-            cast(0, 0, t)
-        q_y(1, 0)
-        mm2(0, 1)
-        il_y(1, 1)
-        turn_y(0, 0, 0)
-        turn_y(0, 0, 1)
-        w(0, 1)
-        q_y(1, 1)
-        make_xs(1, 0)
-        for t in range(4):
-            add2(0, 1, t)
-            cast(0, 1, t)
-        make_xs(1, 1)
-        q_o(0, 0)
-        turn_y(0, 1, 0)
-        turn_y(0, 1, 1)
-        mm2(1, 0)
-        w(1, 0)
-        q_o(0, 1)
-        for t in range(4):
-            add2(1, 0, t)
-            cast(1, 0, t)
-            if t == 1:
-                mm2(1, 1, (0, 1))
-                turn_y(1, 0, 0)
-        mm2(1, 1, (2, 3))
-        turn_y(1, 0, 1)
-        w(1, 1)
-        for t in range(4):
-            add2(1, 1, t)
-            cast(1, 1, t)
-            if t % 2:
-                turn_y(1, 1, t // 2)
-            if t == 1:
-                q_o(1, 0)
-        q_o(1, 1)
+        def each(step, *where, ts=ALL_T):
+            for t in ts:
+                step(*where, t)
+
+
+        gain_x(0, 0)
+        gain_x(0, 1)
+        each(turn_h, 1, 0, ts=PAIRS)
+        start_total(0, 0)
+        weave_x(1, 0, nc.vector.tensor_copy)
+        weave_x(0, 0, nc.vector.tensor_copy)
+        start_total(0, 1)
+        quantize_x(1, 0)
+        gain_x(1, 0)
+        gain_x(1, 1)
+        weave_x(0, 1, nc.vector.tensor_copy)
+        quantize_x(0, 1)
+        each(copy_h, 1, 0, ts=PAIRS)
+        start_total(1, 0)
+        each(turn_h, 0, 0, ts=PAIRS)
+        each(copy_h, 0, 0, ts=PAIRS)
+        turn_h(1, 1, 0)
+        quantize_x(0, 0)
+        each(turn_h, 0, 1, ts=PAIRS)
+        quantize_h(0, 0)
+        each(copy_h, 0, 1, ts=PAIRS)
+        quantize_h(1, 0)
+        quantize_h(0, 1)
+        weave_x(1, 1, nc.scalar.copy)
+
+        each(first_product, 0, 0)
+        turn_h(1, 1, 1)
+        each(first_sum, 0, 0)
+        quantize_x(1, 1)
+        each(copy_h, 1, 1, ts=PAIRS)
+        each(gain_z, 0, 0)
+        weave_y(0, 0)
+        quantize_h(1, 1)
+        each(first_product, 0, 1)
+        each(first_sum, 0, 1)
+        each(gain_z, 0, 1)
+        each(first_product, 1, 0)
+        each(first_sum, 1, 0)
+        each(extend_total, 0, ts=(0, 1))
+        start_total(1, 1)
+        each(first_product, 1, 1)
+        each(gain_z, 1, 0)
+        weave_y(0, 1)
+        each(first_sum, 1, 1)
+        each(extend_total, 1)
+        quantize_y(0, 0)
+        quantize_y(0, 1)
+        each(extend_total, 0, ts=(2, 3))
+        each(gain_z, 1, 1)
+
+        each(second_product, 0, 0)
+        weave_y(1, 0)
+        weave_y(1, 1)
+        each(finish, 0, 0)
+        for t in ALL_T:
+            round_out(0, 0, t, "scalar")
+        each(second_product, 0, 1)
+        quantize_y(1, 0)
+        quantize_y(1, 1)
+        each(second_product, 1, 0)
+        each(finish, 0, 1)
+        each(turn_out, 0, 0, ts=PAIRS)
+        each(finish, 1, 0)
+        for t in ALL_T:
+            round_out(0, 1, t, "scalar")
+        each(copy_out, 0, 0, ts=PAIRS)
+        each(second_product, 1, 1, ts=(0, 1, 2))
+        for t in ALL_T:
+            round_out(1, 0, t, "gpsimd" if t < 2 else "scalar")
+        each(turn_out, 1, 0, ts=PAIRS)
+        second_product(1, 1, 3)
+        each(finish, 1, 1)
+        for t in ALL_T:
+            round_out(1, 1, t, "gpsimd" if t < 3 else "vector")
+        each(turn_out, 0, 1, ts=PAIRS)
+        each(turn_out, 1, 1, ts=PAIRS)
+        each(copy_out, 1, 0, ts=PAIRS)
+        each(copy_out, 0, 1, ts=PAIRS)
+        quantize_out(1, 0, nc.sync)
+        each(copy_out, 1, 1, ts=PAIRS)
+        quantize_out(0, 0, nc.sync)
+        quantize_out(0, 1, nc.sync)
+        quantize_out(1, 1, nc.scalar)

import concourse.mybir as mybir
from concourse.masks import make_identity

F32 = mybir.dt.float32
BF16 = mybir.dt.bfloat16
U32 = mybir.dt.uint32
I32 = mybir.dt.int32
U8 = mybir.dt.uint8
FP8X4 = mybir.dt.float8_e4m3fn_x4
ADD = mybir.AluOpType.add
MULT = mybir.AluOpType.mult
SUB = mybir.AluOpType.subtract
COPY = mybir.ActivationFunctionType.Copy

N = 1024
P = 128
HALF = 512

C_SHIFT = 0.75
E_WIDTH = 1.75
S1 = E_WIDTH / (-2.3 - C_SHIFT)
S2 = 1.0 / (2.0 / S1 - S1)
A = S1 / E_WIDTH
B = 2.0 * S2 / E_WIDTH
D = -S1 * S2

FLOPS = 2 * 2 * N * N * N

ALL_T = (0, 1, 2, 3)
PAIRS = (0, 1)


def tile_chebyshevfilteredsubspaceblock_x1_kernel(tc, h, g, v, x, out, words, scales):
    nc = tc.nc
    with tc.tile_pool(name="keep", bufs=1) as keep, tc.tile_pool(name="work", bufs=3) as work, tc.psum_pool(
        name="bank", bufs=8
    ) as bank, tc.manual_schedule():
        x_raw, x_gain, x_woven, x_codes, x_scales = {}, {}, {}, {}, {}
        h_raw, h_bank, h_woven, h_codes, h_scales = {}, {}, {}, {}, {}
        bank1, z, z_gain, y_woven, y_codes, y_scales = {}, {}, {}, {}, {}, {}
        bank2, total, rounded, p_bank, p_woven, p_scales = {}, {}, {}, {}, {}, {}

        def columns(half):
            return slice(HALF * half, HALF * half + HALF)

        def rows(group):
            return slice(512 * group, 512 * group + 512)


        g_rows = keep.tile([P, 2, 16], BF16, name="g_rows")
        v_rows = keep.tile([P, 2, 16], BF16, name="v_rows")

        def load_x(group, pair):
            if group not in x_raw:
                x_raw[group] = keep.tile([P, 4, N], BF16, name=f"x_raw{group}", align_bytes=64)
            two = slice(2 * pair, 2 * pair + 2)
            nc.sync.dma_start(
                out=x_raw[group][:, two, :], in_=x[rows(group), :].rearrange("(p t) c -> p t c", t=4)[:, two, :]
            )

        def load_h(group, pair):
            h_raw[group, pair] = keep.tile([P, 2, N], BF16, name=f"h_raw{group}{pair}", align_bytes=64)
            nc.sync.dma_start(
                out=h_raw[group, pair][:],
                in_=h[rows(group), :].rearrange("(p t) k -> p t k", t=4)[:, 2 * pair : 2 * pair + 2, :],
            )

        nc.scalar.dma_start(out=g_rows[:, :, 0:4], in_=g.rearrange("(G p t) -> p G t", p=P, t=4))
        load_x(0, 0)
        load_x(0, 1)
        load_h(1, 0)
        load_h(0, 0)
        load_x(1, 0)
        load_x(1, 1)
        load_h(1, 1)
        load_h(0, 1)
        nc.sync.dma_start(out=v_rows[:, :, 0:4], in_=v.rearrange("(G p t) -> p G t", p=P, t=4))


        ag = keep.tile([P, 2, 4], F32, name="ag")
        u = keep.tile([P, 2, 4], F32, name="u")
        abu = keep.tile([P, 2, 4], F32, name="abu")
        identity = keep.tile([P, P], F32, name="identity")
        make_identity(nc, identity[:])
        nc.gpsimd.tensor_scalar(out=ag[:], in0=g_rows[:, :, 0:4], scalar1=A, scalar2=0.0, op0=MULT, op1=ADD)
        nc.gpsimd.tensor_scalar(out=u[:], in0=v_rows[:, :, 0:4], scalar1=C_SHIFT, scalar2=0.0, op0=SUB, op1=ADD)
        nc.gpsimd.tensor_scalar(out=abu[:], in0=u[:], scalar1=A * B, scalar2=0.0, op0=MULT, op1=ADD)


        def quantize(source, name):
            codes = keep.tile([P, 512], U32, name=f"codes_{name}", align_bytes=64)
            scale = keep.tile([P, 512], U8, name=f"scales_{name}", align_bytes=64)
            nc.vector.quantize_mx(out=codes[:].bitcast(FP8X4), scales=scale[:], in_=source)
            return codes, scale

        def weave(copy, woven, source):
            copy(
                out=woven[:].rearrange("p (c i) t -> p c t i", i=4),
                in_=source.rearrange("p t (c i) -> p c t i", i=4),
            )

        def gain_x(group, pair):
            if group not in x_gain:
                x_gain[group] = keep.tile([P, 4, N], BF16, name=f"x_gain{group}", align_bytes=64)
            for t in (2 * pair, 2 * pair + 1):
                nc.vector.tensor_scalar_mul(
                    out=x_gain[group][:, t, :], in0=x_raw[group][:, t, :], scalar1=g_rows[:, group, t : t + 1]
                )

        def weave_x(half, group, copy):
            x_woven[half, group] = work.tile([P, HALF, 4], BF16, name="x_woven", align_bytes=64)
            weave(copy, x_woven[half, group], x_gain[group][:, :, columns(half)])

        def quantize_x(half, group):
            x_codes[half, group], x_scales[half, group] = quantize(
                x_woven[half, group][:].rearrange("p c t -> p (c t)"), f"x{half}{group}"
            )

        def start_total(group, pair):
            if group not in total:
                total[group] = keep.tile([P, 4, N], F32, name=f"total{group}")
            two = slice(2 * pair, 2 * pair + 2)
            nc.scalar.activation(out=total[group][:, two, :], in_=x_raw[group][:, two, :], func=COPY, scale=D)

        def turn_h(group, pair, i):
            row_words = h_raw[group, pair][:, i, :].bitcast(F32)
            turned = bank.tile([P, 512], F32, name="bank")
            h_bank[group, pair, i] = turned
            for k_group in range(2):
                for w in range(2):
                    at = 256 * k_group + 128 * w
                    nc.tensor.transpose(
                        turned[:, at : at + P],
                        row_words[:, 256 * k_group + w : 256 * k_group + 256 : 2],
                        identity[:],
                    )

        def copy_h(group, pair, i):
            if (group, pair) not in h_woven:
                h_woven[group, pair] = work.tile([P, 2, 2, P, 4], BF16, name="h_woven", align_bytes=64)
            nc.scalar.copy(
                out=h_woven[group, pair][:].bitcast(F32)[:, i, :, :, :],
                in_=h_bank[group, pair, i][:].rearrange("p (k w r) -> p k r w", k=2, w=2),
            )

        def quantize_h(group, pair):
            h_codes[group, pair], h_scales[group, pair] = quantize(
                h_woven[group, pair][:].rearrange("p i k r t -> p (i k r t)"), f"h{group}{pair}"
            )

        def product(half, group, t, codes, scale):
            acc = bank.tile([P, HALF], F32, name="bank")
            pair, i = divmod(t, 2)
            for k_group in range(2):
                at = 256 * i + 128 * k_group
                nc.tensor.matmul_mx(
                    out=acc[:],
                    lhsT=h_codes[group, pair][:, at : at + P].bitcast(FP8X4),
                    lhsT_scale=h_scales[group, pair][:, at : at + P],
                    rhs=codes[half, k_group][:].bitcast(FP8X4),
                    rhs_scale=scale[half, k_group][:],
                    start=(k_group == 0),
                    stop=(k_group == 1),
                )
            return acc

        def first_product(half, group, t):
            bank1[half, group, t] = product(half, group, t, x_codes, x_scales)

        def first_sum(half, group, t):
            if group not in z:
                z[group] = keep.tile([P, 4, N], F32, name=f"z{group}")
            nc.vector.scalar_tensor_tensor(
                out=z[group][:, t, columns(half)],
                in0=x_raw[group][:, t, columns(half)],
                scalar=u[:, group, t : t + 1],
                in1=bank1[half, group, t][:],
                op0=MULT,
                op1=ADD,
            )

        def gain_z(half, group, t):
            if (half, group) not in z_gain:
                z_gain[half, group] = work.tile([P, 4, HALF], BF16, name="z_gain", align_bytes=64)
            nc.scalar.activation(
                out=z_gain[half, group][:, t, :],
                in_=z[group][:, t, columns(half)],
                func=COPY,
                scale=ag[:, group, t : t + 1],
            )

        def weave_y(half, group):
            y_woven[half, group] = work.tile([P, HALF, 4], BF16, name="y_woven", align_bytes=64)
            weave(nc.scalar.copy, y_woven[half, group], z_gain[half, group][:])

        def quantize_y(half, group):
            y_codes[half, group], y_scales[half, group] = quantize(
                y_woven[half, group][:].rearrange("p c t -> p (c t)"), f"y{half}{group}"
            )

        def extend_total(group, t):
            nc.vector.scalar_tensor_tensor(
                out=total[group][:, t, :],
                in0=z[group][:, t, :],
                scalar=abu[:, group, t : t + 1],
                in1=total[group][:, t, :],
                op0=MULT,
                op1=ADD,
            )

        def second_product(half, group, t):
            bank2[half, group, t] = product(half, group, t, y_codes, y_scales)

        def finish(half, group, t):
            result = total[group][:, t, columns(half)]
            nc.vector.scalar_tensor_tensor(
                out=result, in0=bank2[half, group, t][:], scalar=B, in1=result, op0=MULT, op1=ADD
            )
            nc.sync.dma_start(
                out=out[rows(group), columns(half)].rearrange("(p t) c -> p t c", t=4)[:, t, :], in_=result
            )

        def round_out(half, group, t, engine):
            rounded[half, group, t] = work.tile([P, 2, P, 2], BF16, name="rounded", bufs=8, align_bytes=64)
            to = rounded[half, group, t][:]
            source = total[group][:, t, columns(half)].rearrange("p (m w e) -> p w m e", w=2, e=2)
            if engine == "gpsimd":
                nc.gpsimd.tensor_scalar(out=to, in0=source, scalar1=1.0, scalar2=0.0, op0=MULT, op1=ADD)
            elif engine == "vector":
                nc.vector.tensor_copy(out=to, in_=source)
            else:
                nc.scalar.copy(out=to, in_=source)

        def turn_out(half, group, pair):
            turned = bank.tile([P, 2, 2, P], F32, name="bank")
            p_bank[half, group, pair] = turned
            for i in range(2):
                pair_words = rounded[half, group, 2 * pair + i][:].rearrange("p w m e -> p (w m e)").bitcast(F32)
                for w in range(2):
                    nc.tensor.transpose(turned[:, i, w, :], pair_words[:, P * w : P * w + P], identity[:])

        def copy_out(half, group, pair):
            if (half, group) not in p_woven:
                p_woven[half, group] = work.tile([P, P, 2, 2, 4], BF16, name="p_woven", bufs=2, align_bytes=64)
            nc.scalar.copy(
                out=p_woven[half, group][:].bitcast(F32)[:, :, pair, :, :],
                in_=p_bank[half, group, pair][:].rearrange("m i w r -> m r i w"),
            )

        def quantize_out(half, group, scale_queue):
            if half not in p_scales:
                p_scales[half] = keep.tile([P, N], U8, name=f"scales_p{half}", align_bytes=64)
            codes = keep.tile([P, 512], U32, name=f"codes_p{half}{group}", align_bytes=64)
            nc.vector.quantize_mx(
                out=codes[:].bitcast(FP8X4),
                scales=p_scales[half][:, rows(group)],
                in_=p_woven[half, group][:].rearrange("m r q i t -> m (r q i t)"),
            )
            nc.sync.dma_start(
                out=words.rearrange("G p r t -> G p (r t)")[half].bitcast(I32)[:, rows(group)],
                in_=codes[:].bitcast(I32),
            )
            if group == 1:
                for q in range(4):
                    scale_queue.dma_start(
                        out=scales[half, 4 * q : 4 * q + 4, :].bitcast(I32),
                        in_=p_scales[half][32 * q : 32 * q + 4, :].bitcast(I32),
                    )

        def each(step, *where, ts=ALL_T):
            for t in ts:
                step(*where, t)


        gain_x(0, 0)
        gain_x(0, 1)
        each(turn_h, 1, 0, ts=PAIRS)
        start_total(0, 0)
        weave_x(1, 0, nc.vector.tensor_copy)
        weave_x(0, 0, nc.vector.tensor_copy)
        start_total(0, 1)
        quantize_x(1, 0)
        gain_x(1, 0)
        gain_x(1, 1)
        weave_x(0, 1, nc.vector.tensor_copy)
        quantize_x(0, 1)
        each(copy_h, 1, 0, ts=PAIRS)
        start_total(1, 0)
        each(turn_h, 0, 0, ts=PAIRS)
        each(copy_h, 0, 0, ts=PAIRS)
        turn_h(1, 1, 0)
        quantize_x(0, 0)
        each(turn_h, 0, 1, ts=PAIRS)
        quantize_h(0, 0)
        each(copy_h, 0, 1, ts=PAIRS)
        quantize_h(1, 0)
        quantize_h(0, 1)
        weave_x(1, 1, nc.scalar.copy)

        each(first_product, 0, 0)
        turn_h(1, 1, 1)
        each(first_sum, 0, 0)
        quantize_x(1, 1)
        each(copy_h, 1, 1, ts=PAIRS)
        each(gain_z, 0, 0)
        weave_y(0, 0)
        quantize_h(1, 1)
        each(first_product, 0, 1)
        each(first_sum, 0, 1)
        each(gain_z, 0, 1)
        each(first_product, 1, 0)
        each(first_sum, 1, 0)
        each(extend_total, 0, ts=(0, 1))
        start_total(1, 1)
        each(first_product, 1, 1)
        each(gain_z, 1, 0)
        weave_y(0, 1)
        each(first_sum, 1, 1)
        each(extend_total, 1)
        quantize_y(0, 0)
        quantize_y(0, 1)
        each(extend_total, 0, ts=(2, 3))
        each(gain_z, 1, 1)

        each(second_product, 0, 0)
        weave_y(1, 0)
        weave_y(1, 1)
        each(finish, 0, 0)
        for t in ALL_T:
            round_out(0, 0, t, "scalar")
        each(second_product, 0, 1)
        quantize_y(1, 0)
        quantize_y(1, 1)
        each(second_product, 1, 0)
        each(finish, 0, 1)
        each(turn_out, 0, 0, ts=PAIRS)
        each(finish, 1, 0)
        for t in ALL_T:
            round_out(0, 1, t, "scalar")
        each(copy_out, 0, 0, ts=PAIRS)
        each(second_product, 1, 1, ts=(0, 1, 2))
        for t in ALL_T:
            round_out(1, 0, t, "gpsimd" if t < 2 else "scalar")
        each(turn_out, 1, 0, ts=PAIRS)
        second_product(1, 1, 3)
        each(finish, 1, 1)
        for t in ALL_T:
            round_out(1, 1, t, "gpsimd" if t < 3 else "vector")
        each(turn_out, 0, 1, ts=PAIRS)
        each(turn_out, 1, 1, ts=PAIRS)
        each(copy_out, 1, 0, ts=PAIRS)
        each(copy_out, 0, 1, ts=PAIRS)
        quantize_out(1, 0, nc.sync)
        each(copy_out, 1, 1, ts=PAIRS)
        quantize_out(0, 0, nc.sync)
        quantize_out(0, 1, nc.sync)
        quantize_out(1, 1, nc.scalar)
